import numpy as np
import ml_dtypes


def mxq(x, axis, fmt="e4m3"):
    dtype, down = {"e4m3": (ml_dtypes.float8_e4m3fn, 7), "e5m2": (ml_dtypes.float8_e5m2, 14)}[fmt]
    v = np.moveaxis(np.asarray(x, np.float32).astype(ml_dtypes.bfloat16).astype(np.float64), axis, -1)
    blocks = v.reshape(v.shape[:-1] + (-1, 32))
    amax = np.abs(blocks).max(-1, keepdims=True)
    byte = np.maximum(np.where(amax > 0, np.frexp(amax)[1] - 1 + 127, 0) - down, 1)
    scale = np.exp2(byte - 127.0)
    codes = (blocks / scale).astype(np.float32).astype(dtype).astype(np.float64)
    return np.moveaxis((codes * scale).reshape(v.shape), -1, axis)


WIDE = False


def mx_kscale(k):
    if not WIDE:
        return np.ones(k)
    levels = np.array([10, -10, 5, -5, 0])
    if k % 512:
        return np.exp2(np.random.permutation(np.resize(levels, k // 32))).repeat(32)
    a = np.empty((k // 512, 16))
    for p in range(k // 512):
        a[p, :8] = np.random.permutation(np.resize(levels, 8))
        for g in range(8):
            far = levels[np.abs(levels - a[p, g]) >= 10]
            a[p, g + 8] = far[np.random.randint(len(far))]
    return np.exp2(a.ravel()).repeat(32)


def f64(x):
    return np.asarray(x).astype(np.float64)


def striped(idx):
    return np.tile(idx.reshape(-1, 16).T, (8, 1)).astype(np.uint16)


def unstriped(offs):
    return offs[:16].T.reshape(-1).astype(np.int64)


def striped8(idx):
    return np.concatenate([x.reshape(-1, 16).T for x in idx]).astype(np.uint16)


def runs(offs, k):
    lists = np.stack([offs[16 * r : 16 * r + 16].T.reshape(-1) for r in range(8)]).astype(np.int64)
    return lists[np.arange(k) % 512 // 64]


def pack_weight(w):
    k, n = w.shape
    w = f64(np.asarray(w, np.float32).astype(ml_dtypes.bfloat16)).reshape(k // 32, 32, n)
    amax = np.abs(w).max(1)
    byte = np.clip(np.where(amax > 0, np.frexp(amax)[1] - 1 + 127 - 7, 1), 1, 254)
    scaled = (w * np.exp2(127.0 - byte)[:, None, :]).reshape(k, n).astype(np.float32)
    words = np.ascontiguousarray(scaled.reshape(k // 512, 128, 4, n).transpose(0, 1, 3, 2)).astype(ml_dtypes.float8_e4m3fn).view(np.uint8)
    return words, np.ascontiguousarray(byte.astype(np.uint8).reshape(k // 512, 16, n))


def unpack_weight(words, scales):
    g, p, n, _ = words.shape
    vals = np.ascontiguousarray(words).view(ml_dtypes.float8_e4m3fn).astype(np.float64) * np.repeat(np.exp2(scales.astype(np.float64) - 127.0), 8, axis=1)[..., None]
    return vals.transpose(0, 1, 3, 2).reshape(g * 512, n)

def planes(y):
    n, m = y.shape
    v = y.astype(np.float32).astype(ml_dtypes.bfloat16).astype(np.float64).reshape(n // 32, 32, m)
    top = np.abs(v).max(1)
    byte = np.clip(np.where(top > 0, np.frexp(top)[1] - 1 + 127 - 7, 1), 1, 254)
    codes = (v * np.exp2(127.0 - byte)[:, None, :]).reshape(n, m).astype(np.float32).astype(ml_dtypes.float8_e4m3fn).view(np.uint8)
    words = codes.reshape(n // 512, 128, 4, m).transpose(0, 1, 3, 2)
    return np.ascontiguousarray(words), np.ascontiguousarray(byte.astype(np.uint8).reshape(n // 512, 16, m))


K, T, S, N, G, H = 512, 1024, 512, 512, 2048, 512


def setup_inputs():
    n = np.random.standard_normal
    s = mx_kscale(K)[:, None]
    u = mx_kscale(S)
    packed_xT = pack_weight(n((K, T)) * s)
    packed_dT = pack_weight(n((K, G)) / s)
    packed_w1 = pack_weight(n((H, N)) / np.sqrt(H) / u[:, None])
    return {
        "x_words": packed_xT[0],
        "x_scales": packed_xT[1],
        "d_words": packed_dT[0],
        "d_scales": packed_dT[1],
        "gn": (np.random.uniform(0.5, 1.5, (H, 1)) * u[:, None]).astype(np.float32),
        "w1_words": packed_w1[0],
        "w1_scales": packed_w1[1],
        "offs": striped(np.random.permutation(T)[:S]),
        "k1": striped8(np.random.randint(0, G, (8, H))),
        "two": striped(np.random.permutation(T)[:S]),
        "k2": striped8(np.random.randint(0, G, (8, H))),
        "n1": striped8(np.stack([np.random.permutation(S) for _ in range(8)])),
        "n2": striped8(np.stack([np.random.permutation(S) for _ in range(8)])),
        "n3": striped8(np.stack([np.random.permutation(S) for _ in range(8)])),
        "n4": striped8(np.stack([np.random.permutation(S) for _ in range(8)])),
    }


def reference(x_words, x_scales, d_words, d_scales, gn, w1_words, w1_scales, offs, k1, two, k2, n1, n2, n3, n4):
    d_k1 = unpack_weight(d_words, d_scales)[np.arange(K)[:, None], runs(k1, K)]
    xq = unpack_weight(x_words, x_scales)[:, unstriped(offs)]
    a = 0.0625 * (d_k1.T @ xq)
    d_k2 = unpack_weight(d_words, d_scales)[np.arange(K)[:, None], runs(k2, K)]
    x_two = unpack_weight(x_words, x_scales)[:, unstriped(two)]
    b = 0.0625 * (d_k2.T @ x_two)
    z = f64(gn) * (a * (np.tanh(b[np.arange(H)[:, None], runs(n1, H)] - (b[np.arange(H)[:, None], runs(n2, H)]))))
    h = unpack_weight(w1_words, w1_scales).T @ mxq(z, 0, "e4m3")
    pa = h[np.arange(N)[:, None], runs(n3, N)]
    pb = h[np.arange(N)[:, None], runs(n4, N)]
    out_0 = np.maximum(np.maximum(h, pa), pb) - (0.5 * (np.minimum(np.minimum(h, pa), pb)))
    return (out_0,) + planes(out_0)

@@ -1,0 +1,257 @@
+from contextlib import ExitStack
+
+import concourse.mybir as mybir
+
+F32 = mybir.dt.float32
+BF16 = mybir.dt.bfloat16
+I32 = mybir.dt.int32
+U32 = mybir.dt.uint32
+U16 = mybir.dt.uint16
+U8 = mybir.dt.uint8
+FP8X4 = mybir.dt.float8_e4m3fn_x4
+ALU = mybir.AluOpType
+ACT = mybir.ActivationFunctionType
+
+P = 128
+PACK = 4
+T, G, S = 1024, 2048, 512
+HALF = S // 2
+FLOPS = 3 * 2 * 512 * 512 * 512
+
+
+def tile_picked_twpqjointbrange_none_po_kernel(
+    tc, x_words, x_scales, d_words, d_scales, gn, w1_words, w1_scales,
+    offs, k1, two, k2, n1, n2, n3, n4, out_0, out_1, out_2,
+):
+    nc = tc.nc
+    with ExitStack() as ctx:
+        keep = ctx.enter_context(tc.tile_pool(name="keep", bufs=1))
+        psum = ctx.enter_context(tc.psum_pool(name="psum", bufs=1))
+
+        def sb(name, shape, dtype, tag=None):
+            return keep.tile(shape, dtype, name=name, tag=tag or name, align_bytes=64)
+
+        def load_list(name, src):
+            lst = keep.tile([P, S // 16], U16, name=name)
+            nc.sync.dma_start(lst[:], src)
+            return lst
+
+        def load_words(name, src, cols, tag=None):
+            words = sb(name, [P, cols], U32, tag)
+            nc.sync.dma_start(words[:].bitcast(I32), src[0].rearrange("p n t -> p (n t)").bitcast(I32))
+            return words
+
+        def load_block_rows(name, src, cols):
+            plane = sb(name, [P, cols], U8)
+            rows = src[0].bitcast(I32).unsqueeze(1).to_broadcast([16, 8, cols // 4])
+            nc.sync.dma_start(plane[:].bitcast(I32), rows)
+            return plane
+
+        k2_t = load_list("k2_t", k2)
+        d_bytes = load_block_rows("d_bytes", d_scales, G)
+        two_t = load_list("two_t", two)
+        x_bytes = load_block_rows("x_bytes", x_scales, T)
+        k1_t = load_list("k1_t", k1)
+        offs_t = load_list("offs_t", offs)
+        x_w = load_words("x_w", x_words, T)
+        d_w = load_words("d_w", d_words, G)
+        n1_t = load_list("n1_t", n1)
+        n2_t = load_list("n2_t", n2)
+        n3_t = load_list("n3_t", n3)
+        n4_t = load_list("n4_t", n4)
+
+        w1_bytes = sb("w1_bytes", [P, S], U8)
+        nc.gpsimd.memset(w1_bytes[:].bitcast(I32), 0)
+        gain_raw = sb("gain_raw", [P, PACK], F32)
+        nc.gpsimd.dma_start(gain_raw[:], gn.rearrange("(p t) o -> p (t o)", t=PACK))
+        for q in range(4):
+            nc.gpsimd.dma_start(w1_bytes[32 * q : 32 * q + 4, :].bitcast(I32), w1_scales[0, 4 * q : 4 * q + 4, :].bitcast(I32))
+        gain = sb("gain", [P, PACK], F32)
+        nc.gpsimd.tensor_scalar(gain[:], gain_raw[:], 0.0625, 0.0, ALU.mult, ALU.add)
+
+        def deal(copy, dst, src):
+            copy(dst.rearrange("p (t m) -> p t m", t=PACK), src.rearrange("p (m t) -> p t m", t=PACK))
+
+        def half_of(lst, c):
+            return lst[:, c * HALF // 16 : (c + 1) * HALF // 16]
+
+        def scale_plane(name, d_list, x_list, tag):
+            picked = sb(name + "_picked", [P, 2 * S], U8, tag)
+            plane = sb(name + "_plane", [P, 2 * S], U8)
+            nc.vector.tensor_copy(picked[:, :S], d_bytes[:].indirect(d_list[:]))
+            nc.vector.tensor_copy(picked[:, S:], x_bytes[:].indirect(x_list[:]))
+            deal(nc.vector.tensor_copy, plane[:, :S], picked[:, :S])
+            nc.vector.tensor_copy(plane[:, S:].bitcast(I32), picked[:, S:].bitcast(I32))
+            for r in range(1, 4):
+                nc.sync.dma_start(plane[r:P:32, :].bitcast(I32), plane[8 * r : P : 32, :].bitcast(I32))
+            return plane
+
+        def products(name, d_dealt, x_picked, plane):
+            banks = []
+            for t in range(PACK):
+                bank = psum.tile([P, S], F32, name=name + "_bank", tag=name + str(t))
+                cols = slice(t * P, (t + 1) * P)
+                nc.tensor.matmul_mx(
+                    bank[:], lhsT=d_dealt[:, cols].bitcast(FP8X4), lhsT_scale=plane[:, cols],
+                    rhs=x_picked.bitcast(FP8X4), rhs_scale=plane[:, S:], start=True, stop=True,
+                )
+                banks.append(bank)
+            return banks
+
+        b_plane = scale_plane("b", k2_t, two_t, "b_picked")
+        w1_w = load_words("w1_w", w1_words, S, "b_picked")
+        b_x = sb("b_x", [P, S], U32)
+        nc.vector.tensor_copy(b_x[:], x_w[:].indirect(two_t[:]))
+        b_dealt = sb("b_dealt", [P, PACK, P], U32)
+        b_d = [sb("b_d" + str(c), [P, HALF], U32) for c in range(2)]
+        for c in range(2):
+            nc.vector.tensor_copy(b_d[c][:], d_w[:].indirect(half_of(k2_t, c)))
+        for c in range(2):
+            nc.vector.tensor_copy(b_dealt[:, :, c * P // 2 : (c + 1) * P // 2], b_d[c][:].rearrange("p (m t) -> p t m", t=PACK))
+        b_banks = products("b", b_dealt[:].rearrange("p t m -> p (t m)"), b_x[:], b_plane)
+
+        w1_dealt = sb("w1_dealt", [P, S], U32)
+        deal(nc.scalar.copy, w1_dealt[:], w1_w[:])
+
+        a_plane = scale_plane("a", k1_t, offs_t, "b_d0")
+        a_words = sb("a_words", [P, 2 * S], U32, "b_d1")
+        a_dealt = sb("a_dealt", [P, S], U32)
+        nc.vector.tensor_copy(a_words[:, :S], d_w[:].indirect(k1_t[:]))
+        nc.vector.tensor_copy(a_words[:, S:], x_w[:].indirect(offs_t[:]))
+        deal(nc.vector.tensor_copy, a_dealt[:], a_words[:, :S])
+        a_banks = products("a", a_dealt[:], a_words[:, S:], a_plane)
+        w1_sdealt = sb("w1_sdealt", [P, S], U8, "b_d0")
+        deal(nc.vector.tensor_copy, w1_sdealt[:], w1_bytes[:])
+
+        def gather_s(dst, window, lst, c):
+            nc.scalar.activation(dst, window[:].indirect(half_of(lst, c)), ACT.Copy)
+
+        def gather_v(dst, window, lst, c):
+            nc.vector.tensor_copy(dst, window[:].indirect(half_of(lst, c)))
+
+        def halves(name, dtype):
+            return [sb(name + str(c), [P, PACK, HALF], dtype) for c in range(2)]
+
+        b_rows = [sb("b_row" + str(t), [P, S], F32) for t in range(PACK)]
+        g1, g2, diff, th = halves("g1_", F32), halves("g2_", F32), halves("diff", F32), halves("th", F32)
+        z_rows = halves("z_rows", BF16)
+        z_woven = [sb("z_woven" + str(c), [P, HALF, PACK], BF16) for c in range(2)]
+        z_codes = [sb("z_codes" + str(c), [P, HALF], U32) for c in range(2)]
+        z_bytes = [sb("z_bytes" + str(c), [P, HALF], U8) for c in range(2)]
+
+        def weave(copy, dst, src):
+            copy(dst.rearrange("p (c i) t -> p c t i", i=4), src.rearrange("p t (c i) -> p c t i", i=4))
+
+        def quantize(codes, plane, woven):
+            nc.vector.quantize_mx(codes.bitcast(FP8X4), plane, woven[:].rearrange("p j t -> p (j t)"))
+
+        def sub_plain(c, t0, t1):
+            nc.vector.tensor_tensor(diff[c][:, t0:t1, :], g1[c][:, t0:t1, :], g2[c][:, t0:t1, :], ALU.subtract)
+
+        def sub_fused(c, t):
+            nc.vector.tensor_tensor(diff[c][:, t, :], b_rows[t][:].indirect(half_of(n1_t, c)), g2[c][:, t, :], ALU.subtract)
+
+        def tanh(c, t0, t1):
+            nc.scalar.activation(th[c][:, t0:t1, :], diff[c][:, t0:t1, :], ACT.Tanh, scale=0.0625)
+
+        def make_z(c, t):
+            nc.vector.scalar_tensor_tensor(
+                z_rows[c][:, t, :], a_banks[t][:, c * HALF : (c + 1) * HALF], gain[:, t : t + 1], th[c][:, t, :],
+                ALU.mult, ALU.mult,
+            )
+
+        h_banks = [[psum.tile([P, 2, HALF], F32, name="h_bank", tag="b" + str(2 * c + u)) for u in range(2)] for c in range(2)]
+        h_rows = [sb("h_row" + str(t), [P, S], F32) for t in range(PACK)]
+
+        def h_product(c):
+            for t in range(PACK):
+                cols = slice(t * P, (t + 1) * P)
+                nc.tensor.matmul_mx(
+                    h_banks[c][t // 2][:, t % 2, :], lhsT=w1_dealt[:, cols].bitcast(FP8X4), lhsT_scale=w1_sdealt[:, cols],
+                    rhs=z_codes[c][:].bitcast(FP8X4), rhs_scale=z_bytes[c][:], start=True, stop=True,
+                )
+
+        def h_out(copy, c, t):
+            copy(h_rows[t][:, c * HALF : (c + 1) * HALF], h_banks[c][t // 2][:, t % 2, :])
+
+        pa, pb = halves("pa", F32), halves("pb", F32)
+        hi2, lo2, hi3, lo3, res = halves("hi2_", F32), halves("lo2_", F32), halves("hi3_", F32), halves("lo3_", F32), halves("res", F32)
+        o_woven = [sb("o_woven" + str(c), [P, HALF, PACK], BF16) for c in range(2)]
+        o_codes = [sb("o_codes" + str(c), [P, HALF], U32) for c in range(2)]
+        o_bytes = sb("o_bytes", [P, S], U8)
+        out_rows = out_0.rearrange("(p t) j -> p t j", t=PACK)
+        out_words = out_1[0].rearrange("p n t -> p (n t)").bitcast(I32)
+
+        def with_h(c, u):
+            ts = slice(2 * u, 2 * u + 2)
+            nc.vector.tensor_tensor(hi2[c][:, ts, :], pa[c][:, ts, :], h_banks[c][u][:], ALU.max)
+            nc.vector.tensor_tensor(lo2[c][:, ts, :], pa[c][:, ts, :], h_banks[c][u][:], ALU.min)
+
+        def finish(c, u):
+            ts = slice(2 * u, 2 * u + 2)
+            nc.vector.tensor_tensor(lo3[c][:, ts, :], lo2[c][:, ts, :], pb[c][:, ts, :], ALU.min)
+            nc.vector.tensor_tensor(hi3[c][:, ts, :], hi2[c][:, ts, :], pb[c][:, ts, :], ALU.max)
+            nc.vector.scalar_tensor_tensor(res[c][:, ts, :], lo3[c][:, ts, :], -0.5, hi3[c][:, ts, :], ALU.mult, ALU.add)
+            nc.sync.dma_start(out_rows[:, ts, c * HALF : (c + 1) * HALF], res[c][:, ts, :])
+
+        def planes_out(c):
+            quantize(o_codes[c][:], o_bytes[:, c * HALF : (c + 1) * HALF], o_woven[c])
+            nc.sync.dma_start(out_words[:, c * HALF : (c + 1) * HALF], o_codes[c][:].bitcast(I32))
+
+        for t in range(PACK):
+            nc.scalar.copy(b_rows[t][:], b_banks[t][:])
+            gather_s(g1[0][:, t, :], b_rows[t], n1_t, 0)
+            gather_s(g2[0][:, t, :], b_rows[t], n2_t, 0)
+        sub_plain(0, 0, 2)
+        for t in range(2):
+            gather_v(g2[1][:, t, :], b_rows[t], n2_t, 1)
+        for t in range(2):
+            sub_fused(1, t)
+        tanh(0, 0, 2)
+        sub_plain(0, 2, 4)
+        tanh(1, 0, 2)
+        gather_s(g2[1][:, 2, :], b_rows[2], n2_t, 1)
+        tanh(0, 2, 4)
+        make_z(0, 0)
+        make_z(0, 1)
+        gather_s(g2[1][:, 3, :], b_rows[3], n2_t, 1)
+        gather_s(g1[1][:, 3, :], b_rows[3], n1_t, 1)
+        sub_fused(1, 2)
+        make_z(0, 2)
+        make_z(0, 3)
+        sub_plain(1, 3, 4)
+        tanh(1, 2, 4)
+        weave(nc.scalar.copy, z_woven[0][:], z_rows[0][:])
+        for t in range(PACK):
+            make_z(1, t)
+        quantize(z_codes[0][:], z_bytes[0][:], z_woven[0])
+        h_product(0)
+        weave(nc.vector.tensor_copy, z_woven[1][:], z_rows[1][:])
+        quantize(z_codes[1][:], z_bytes[1][:], z_woven[1])
+        for t in range(PACK):
+            h_out(nc.scalar.copy, 0, t)
+        h_product(1)
+
+        for c in range(2):
+            for u in range(2):
+                for t in (2 * u, 2 * u + 1):
+                    if c == 0:
+                        h_out(nc.scalar.copy, 1, t)
+                    if c == 0 and u == 0:
+                        gather_v(pa[c][:, t, :], h_rows[t], n3_t, c)
+                    else:
+                        gather_s(pa[c][:, t, :], h_rows[t], n3_t, c)
+                with_h(c, u)
+                for t in (2 * u, 2 * u + 1):
+                    gather_s(pb[c][:, t, :], h_rows[t], n4_t, c)
+                if c == 1 and u == 0:
+                    weave(nc.scalar.copy, o_woven[0][:], res[0][:])
+                if c == 1 and u == 1:
+                    planes_out(0)
+                finish(c, u)
+        weave(nc.scalar.copy, o_woven[1][:, :96, :], res[1][:, :, :96])
+        weave(nc.vector.tensor_copy, o_woven[1][:, 96:, :], res[1][:, :, 96:])
+        planes_out(1)
+        for q in range(4):
+            queue = nc.sync if q % 2 == 0 else nc.scalar
+            queue.dma_start(out_2[0, 4 * q : 4 * q + 4, :].bitcast(I32), o_bytes[32 * q : 32 * q + 4, :].bitcast(I32))

@@ -16,6 +16,9 @@ P = 128
 PACK = 4
 T, G, S = 1024, 2048, 512
 HALF = S // 2
+STARTS = (0, 256, 384)
+WIDTHS = (256, 128, 128)
+UNITS = ((0, 0, 2), (0, 2, 4), (1, 0, 4), (2, 0, 4))
 FLOPS = 3 * 2 * 512 * 512 * 512
 
 
@@ -47,10 +50,10 @@ def tile_picked_twpqjointbrange_none_po_kernel(
             nc.sync.dma_start(plane[:].bitcast(I32), rows)
             return plane
 
-        k2_t = load_list("k2_t", k2)
-        d_bytes = load_block_rows("d_bytes", d_scales, G)
         two_t = load_list("two_t", two)
         x_bytes = load_block_rows("x_bytes", x_scales, T)
+        k2_t = load_list("k2_t", k2)
+        d_bytes = load_block_rows("d_bytes", d_scales, G)
         k1_t = load_list("k1_t", k1)
         offs_t = load_list("offs_t", offs)
         x_w = load_words("x_w", x_words, T)
@@ -60,17 +63,12 @@ def tile_picked_twpqjointbrange_none_po_kernel(
         n3_t = load_list("n3_t", n3)
         n4_t = load_list("n4_t", n4)
 
-        w1_bytes = sb("w1_bytes", [P, S], U8)
-        nc.gpsimd.memset(w1_bytes[:].bitcast(I32), 0)
-        gain_raw = sb("gain_raw", [P, PACK], F32)
-        nc.gpsimd.dma_start(gain_raw[:], gn.rearrange("(p t) o -> p (t o)", t=PACK))
-        for q in range(4):
-            nc.gpsimd.dma_start(w1_bytes[32 * q : 32 * q + 4, :].bitcast(I32), w1_scales[0, 4 * q : 4 * q + 4, :].bitcast(I32))
-        gain = sb("gain", [P, PACK], F32)
-        nc.gpsimd.tensor_scalar(gain[:], gain_raw[:], 0.0625, 0.0, ALU.mult, ALU.add)
 
         def deal(copy, dst, src):
             copy(dst.rearrange("p (t m) -> p t m", t=PACK), src.rearrange("p (m t) -> p t m", t=PACK))
+
+        def deal_words(copy, dst, src):
+            copy(dst.rearrange("p t m -> p m t"), src.rearrange("p (m t) -> p m t", t=PACK))
 
         def half_of(lst, c):
             return lst[:, c * HALF // 16 : (c + 1) * HALF // 16]
@@ -78,10 +76,10 @@ def tile_picked_twpqjointbrange_none_po_kernel(
         def scale_plane(name, d_list, x_list, tag):
             picked = sb(name + "_picked", [P, 2 * S], U8, tag)
             plane = sb(name + "_plane", [P, 2 * S], U8)
-            nc.vector.tensor_copy(picked[:, :S], d_bytes[:].indirect(d_list[:]))
             nc.vector.tensor_copy(picked[:, S:], x_bytes[:].indirect(x_list[:]))
-            deal(nc.vector.tensor_copy, plane[:, :S], picked[:, :S])
+            nc.vector.tensor_copy(picked[:, :S], d_bytes[:].indirect(d_list[:]))
             nc.vector.tensor_copy(plane[:, S:].bitcast(I32), picked[:, S:].bitcast(I32))
+            deal(nc.vector.tensor_copy, plane[:, :S], picked[:, :S])
             for r in range(1, 4):
                 nc.sync.dma_start(plane[r:P:32, :].bitcast(I32), plane[8 * r : P : 32, :].bitcast(I32))
             return plane
@@ -107,37 +105,49 @@ def tile_picked_twpqjointbrange_none_po_kernel(
         for c in range(2):
             nc.vector.tensor_copy(b_d[c][:], d_w[:].indirect(half_of(k2_t, c)))
         for c in range(2):
-            nc.vector.tensor_copy(b_dealt[:, :, c * P // 2 : (c + 1) * P // 2], b_d[c][:].rearrange("p (m t) -> p t m", t=PACK))
+            deal_words(nc.vector.tensor_copy, b_dealt[:, :, c * P // 2 : (c + 1) * P // 2], b_d[c][:])
         b_banks = products("b", b_dealt[:].rearrange("p t m -> p (t m)"), b_x[:], b_plane)
 
-        w1_dealt = sb("w1_dealt", [P, S], U32)
-        deal(nc.scalar.copy, w1_dealt[:], w1_w[:])
+
+        w1_bytes = sb("w1_bytes", [P, S], U8, "b_x")
+        nc.gpsimd.memset(w1_bytes[:].bitcast(I32), 0)
+        for q in range(4):
+            nc.sync.dma_start(w1_bytes[32 * q : 32 * q + 4, :].bitcast(I32), w1_scales[0, 4 * q : 4 * q + 4, :].bitcast(I32))
+        gain_raw = sb("gain_raw", [P, PACK], F32, "b_dealt")
+        nc.sync.dma_start(gain_raw[:], gn.rearrange("(p t) o -> p (t o)", t=PACK))
+        gain = sb("gain", [P, PACK], F32)
+        nc.gpsimd.tensor_scalar(gain[:], gain_raw[:], 0.0625, 0.0, ALU.mult, ALU.add)
 
         a_plane = scale_plane("a", k1_t, offs_t, "b_d0")
         a_words = sb("a_words", [P, 2 * S], U32, "b_d1")
         a_dealt = sb("a_dealt", [P, S], U32)
         nc.vector.tensor_copy(a_words[:, :S], d_w[:].indirect(k1_t[:]))
         nc.vector.tensor_copy(a_words[:, S:], x_w[:].indirect(offs_t[:]))
-        deal(nc.vector.tensor_copy, a_dealt[:], a_words[:, :S])
+        deal_words(nc.vector.tensor_copy, a_dealt[:].rearrange("p (t m) -> p t m", t=PACK), a_words[:, :S])
         a_banks = products("a", a_dealt[:], a_words[:, S:], a_plane)
-        w1_sdealt = sb("w1_sdealt", [P, S], U8, "b_d0")
-        deal(nc.vector.tensor_copy, w1_sdealt[:], w1_bytes[:])
+
+        def cols_of(c):
+            return slice(STARTS[c], STARTS[c] + WIDTHS[c])
+
+        def entries(lst, c):
+            return lst[:, STARTS[c] // 16 : (STARTS[c] + WIDTHS[c]) // 16]
 
         def gather_s(dst, window, lst, c):
-            nc.scalar.activation(dst, window[:].indirect(half_of(lst, c)), ACT.Copy)
+            nc.scalar.activation(dst, window[:].indirect(entries(lst, c)), ACT.Copy)
 
         def gather_v(dst, window, lst, c):
-            nc.vector.tensor_copy(dst, window[:].indirect(half_of(lst, c)))
+            nc.vector.tensor_copy(dst, window[:].indirect(entries(lst, c)))
 
-        def halves(name, dtype):
-            return [sb(name + str(c), [P, PACK, HALF], dtype) for c in range(2)]
+        def by_chunk(name, dtype):
+            return [sb(name + str(c), [P, PACK, WIDTHS[c]], dtype) for c in range(3)]
 
         b_rows = [sb("b_row" + str(t), [P, S], F32) for t in range(PACK)]
-        g1, g2, diff, th = halves("g1_", F32), halves("g2_", F32), halves("diff", F32), halves("th", F32)
-        z_rows = halves("z_rows", BF16)
-        z_woven = [sb("z_woven" + str(c), [P, HALF, PACK], BF16) for c in range(2)]
-        z_codes = [sb("z_codes" + str(c), [P, HALF], U32) for c in range(2)]
-        z_bytes = [sb("z_bytes" + str(c), [P, HALF], U8) for c in range(2)]
+        g1 = by_chunk("g1_", F32)
+        g2, diff, th = by_chunk("g2_", F32), by_chunk("diff", F32), by_chunk("th", F32)
+        z_rows = by_chunk("z_rows", BF16)
+        z_woven = [sb("z_woven" + str(c), [P, WIDTHS[c], PACK], BF16) for c in range(3)]
+        z_codes = [sb("z_codes" + str(c), [P, WIDTHS[c]], U32) for c in range(3)]
+        z_bytes = [sb("z_bytes" + str(c), [P, WIDTHS[c]], U8) for c in range(3)]
 
         def weave(copy, dst, src):
             copy(dst.rearrange("p (c i) t -> p c t i", i=4), src.rearrange("p t (c i) -> p c t i", i=4))
@@ -145,113 +155,124 @@ def tile_picked_twpqjointbrange_none_po_kernel(
         def quantize(codes, plane, woven):
             nc.vector.quantize_mx(codes.bitcast(FP8X4), plane, woven[:].rearrange("p j t -> p (j t)"))
 
-        def sub_plain(c, t0, t1):
-            nc.vector.tensor_tensor(diff[c][:, t0:t1, :], g1[c][:, t0:t1, :], g2[c][:, t0:t1, :], ALU.subtract)
-
         def sub_fused(c, t):
-            nc.vector.tensor_tensor(diff[c][:, t, :], b_rows[t][:].indirect(half_of(n1_t, c)), g2[c][:, t, :], ALU.subtract)
+            nc.vector.tensor_tensor(diff[c][:, t, :], b_rows[t][:].indirect(entries(n1_t, c)), g2[c][:, t, :], ALU.subtract)
 
         def tanh(c, t0, t1):
             nc.scalar.activation(th[c][:, t0:t1, :], diff[c][:, t0:t1, :], ACT.Tanh, scale=0.0625)
 
-        def make_z(c, t):
-            nc.vector.scalar_tensor_tensor(
-                z_rows[c][:, t, :], a_banks[t][:, c * HALF : (c + 1) * HALF], gain[:, t : t + 1], th[c][:, t, :],
-                ALU.mult, ALU.mult,
-            )
+        def make_z(c, t0, t1):
+            for t in range(t0, t1):
+                nc.vector.scalar_tensor_tensor(
+                    z_rows[c][:, t, :], a_banks[t][:, cols_of(c)], gain[:, t : t + 1], th[c][:, t, :], ALU.mult, ALU.mult,
+                )
 
-        h_banks = [[psum.tile([P, 2, HALF], F32, name="h_bank", tag="b" + str(2 * c + u)) for u in range(2)] for c in range(2)]
+        h_banks = [psum.tile([P, t1 - t0, WIDTHS[c]], F32, name="h_bank", tag="b" + str(u)) for u, (c, t0, t1) in enumerate(UNITS)]
         h_rows = [sb("h_row" + str(t), [P, S], F32) for t in range(PACK)]
 
+        def h_psum(c, t):
+            u = [k for k, (cc, t0, t1) in enumerate(UNITS) if cc == c and t0 <= t < t1][0]
+            return h_banks[u][:, t - UNITS[u][1], :]
+
         def h_product(c):
+            quantize(z_codes[c][:], z_bytes[c][:], z_woven[c])
             for t in range(PACK):
                 cols = slice(t * P, (t + 1) * P)
                 nc.tensor.matmul_mx(
-                    h_banks[c][t // 2][:, t % 2, :], lhsT=w1_dealt[:, cols].bitcast(FP8X4), lhsT_scale=w1_sdealt[:, cols],
+                    h_psum(c, t), lhsT=w1_dealt[:, cols].bitcast(FP8X4), lhsT_scale=w1_sdealt[:, cols],
                     rhs=z_codes[c][:].bitcast(FP8X4), rhs_scale=z_bytes[c][:], start=True, stop=True,
                 )
 
-        def h_out(copy, c, t):
-            copy(h_rows[t][:, c * HALF : (c + 1) * HALF], h_banks[c][t // 2][:, t % 2, :])
+        def h_out(c, t):
+            nc.scalar.copy(h_rows[t][:, cols_of(c)], h_psum(c, t))
 
-        pa, pb = halves("pa", F32), halves("pb", F32)
-        hi2, lo2, hi3, lo3, res = halves("hi2_", F32), halves("lo2_", F32), halves("hi3_", F32), halves("lo3_", F32), halves("res", F32)
-        o_woven = [sb("o_woven" + str(c), [P, HALF, PACK], BF16) for c in range(2)]
-        o_codes = [sb("o_codes" + str(c), [P, HALF], U32) for c in range(2)]
+        pa, pb = by_chunk("pa", F32), by_chunk("pb", F32)
+        hi2, lo2, hi3, lo3, res = [by_chunk(n, F32) for n in ("hi2_", "lo2_", "hi3_", "lo3_", "res")]
+        o_woven = [sb("o_woven" + str(c), [P, WIDTHS[c], PACK], BF16) for c in range(3)]
+        o_codes = [sb("o_codes" + str(c), [P, WIDTHS[c]], U32) for c in range(3)]
         o_bytes = sb("o_bytes", [P, S], U8)
         out_rows = out_0.rearrange("(p t) j -> p t j", t=PACK)
         out_words = out_1[0].rearrange("p n t -> p (n t)").bitcast(I32)
 
-        def with_h(c, u):
-            ts = slice(2 * u, 2 * u + 2)
-            nc.vector.tensor_tensor(hi2[c][:, ts, :], pa[c][:, ts, :], h_banks[c][u][:], ALU.max)
-            nc.vector.tensor_tensor(lo2[c][:, ts, :], pa[c][:, ts, :], h_banks[c][u][:], ALU.min)
+        def with_h(u):
+            c, t0, t1 = UNITS[u]
+            nc.vector.tensor_tensor(hi2[c][:, t0:t1, :], pa[c][:, t0:t1, :], h_banks[u][:], ALU.max)
+            nc.vector.tensor_tensor(lo2[c][:, t0:t1, :], pa[c][:, t0:t1, :], h_banks[u][:], ALU.min)
 
-        def finish(c, u):
-            ts = slice(2 * u, 2 * u + 2)
-            nc.vector.tensor_tensor(lo3[c][:, ts, :], lo2[c][:, ts, :], pb[c][:, ts, :], ALU.min)
-            nc.vector.tensor_tensor(hi3[c][:, ts, :], hi2[c][:, ts, :], pb[c][:, ts, :], ALU.max)
-            nc.vector.scalar_tensor_tensor(res[c][:, ts, :], lo3[c][:, ts, :], -0.5, hi3[c][:, ts, :], ALU.mult, ALU.add)
-            nc.sync.dma_start(out_rows[:, ts, c * HALF : (c + 1) * HALF], res[c][:, ts, :])
+        def finish(c, t0, t1, engine):
+            nc.vector.tensor_tensor(lo3[c][:, t0:t1, :], lo2[c][:, t0:t1, :], pb[c][:, t0:t1, :], ALU.min)
+            nc.vector.tensor_tensor(hi3[c][:, t0:t1, :], hi2[c][:, t0:t1, :], pb[c][:, t0:t1, :], ALU.max)
+            nc.vector.scalar_tensor_tensor(res[c][:, t0:t1, :], lo3[c][:, t0:t1, :], -0.5, hi3[c][:, t0:t1, :], ALU.mult, ALU.add)
+            nc.sync.dma_start(out_rows[:, t0:t1, cols_of(c)], res[c][:, t0:t1, :])
 
         def planes_out(c):
-            quantize(o_codes[c][:], o_bytes[:, c * HALF : (c + 1) * HALF], o_woven[c])
-            nc.sync.dma_start(out_words[:, c * HALF : (c + 1) * HALF], o_codes[c][:].bitcast(I32))
+            quantize(o_codes[c][:], o_bytes[:, cols_of(c)], o_woven[c])
+            nc.sync.dma_start(out_words[:, cols_of(c)], o_codes[c][:].bitcast(I32))
 
         for t in range(PACK):
             nc.scalar.copy(b_rows[t][:], b_banks[t][:])
-            gather_s(g1[0][:, t, :], b_rows[t], n1_t, 0)
             gather_s(g2[0][:, t, :], b_rows[t], n2_t, 0)
-        sub_plain(0, 0, 2)
-        for t in range(2):
-            gather_v(g2[1][:, t, :], b_rows[t], n2_t, 1)
-        for t in range(2):
+            if t == 0:
+                gather_s(g1[0][:, t, :], b_rows[t], n1_t, 0)
+        nc.vector.tensor_tensor(diff[0][:, 0, :], g1[0][:, 0, :], g2[0][:, 0, :], ALU.subtract)
+        for t in range(1, PACK):
+            sub_fused(0, t)
+        for t in range(PACK):
+            gather_s(g2[1][:, t, :], b_rows[t], n2_t, 1)
             sub_fused(1, t)
+        w1_sdealt = sb("w1_sdealt", [P, S], U8, "g1_0")
+        deal(nc.vector.tensor_copy, w1_sdealt[:], w1_bytes[:])
         tanh(0, 0, 2)
-        sub_plain(0, 2, 4)
-        tanh(1, 0, 2)
-        gather_s(g2[1][:, 2, :], b_rows[2], n2_t, 1)
         tanh(0, 2, 4)
-        make_z(0, 0)
-        make_z(0, 1)
-        gather_s(g2[1][:, 3, :], b_rows[3], n2_t, 1)
-        gather_s(g1[1][:, 3, :], b_rows[3], n1_t, 1)
-        sub_fused(1, 2)
-        make_z(0, 2)
-        make_z(0, 3)
-        sub_plain(1, 3, 4)
-        tanh(1, 2, 4)
-        weave(nc.scalar.copy, z_woven[0][:], z_rows[0][:])
+        make_z(0, 0, 4)
         for t in range(PACK):
-            make_z(1, t)
-        quantize(z_codes[0][:], z_bytes[0][:], z_woven[0])
+            gather_s(g2[2][:, t, :], b_rows[t], n2_t, 2)
+            gather_s(g1[2][:, t, :], b_rows[t], n1_t, 2)
+            if t == 1:
+                tanh(1, 0, 4)
+            if t % 2 == 1:
+                nc.vector.tensor_tensor(diff[2][:, t - 1 : t + 1, :], g1[2][:, t - 1 : t + 1, :], g2[2][:, t - 1 : t + 1, :], ALU.subtract)
+        weave(nc.vector.tensor_copy, z_woven[0][:], z_rows[0][:])
+        w1_dealt = sb("w1_dealt", [P, S], U32, "g2_1")
+        deal_words(nc.scalar.copy, w1_dealt[:].rearrange("p (t m) -> p t m", t=PACK), w1_w[:])
         h_product(0)
+        make_z(1, 0, 4)
+        tanh(2, 0, 2)
+        tanh(2, 2, 4)
         weave(nc.vector.tensor_copy, z_woven[1][:], z_rows[1][:])
-        quantize(z_codes[1][:], z_bytes[1][:], z_woven[1])
-        for t in range(PACK):
-            h_out(nc.scalar.copy, 0, t)
         h_product(1)
+        make_z(2, 0, 4)
+        weave(nc.vector.tensor_copy, z_woven[2][:], z_rows[2][:])
+        h_product(2)
+        for t in range(PACK):
+            h_out(0, t)
 
-        for c in range(2):
-            for u in range(2):
-                for t in (2 * u, 2 * u + 1):
-                    if c == 0:
-                        h_out(nc.scalar.copy, 1, t)
-                    if c == 0 and u == 0:
-                        gather_v(pa[c][:, t, :], h_rows[t], n3_t, c)
+        for u, (c, t0, t1) in enumerate(UNITS):
+            for t in range(t0, t1):
+                if c == 0:
+                    h_out(1, t)
+                    if u == 0:
+                        nc.vector.tensor_copy(h_rows[t][:, cols_of(2)], h_psum(2, t))
                     else:
-                        gather_s(pa[c][:, t, :], h_rows[t], n3_t, c)
-                with_h(c, u)
-                for t in (2 * u, 2 * u + 1):
-                    gather_s(pb[c][:, t, :], h_rows[t], n4_t, c)
-                if c == 1 and u == 0:
-                    weave(nc.scalar.copy, o_woven[0][:], res[0][:])
-                if c == 1 and u == 1:
-                    planes_out(0)
-                finish(c, u)
-        weave(nc.scalar.copy, o_woven[1][:, :96, :], res[1][:, :, :96])
-        weave(nc.vector.tensor_copy, o_woven[1][:, 96:, :], res[1][:, :, 96:])
+                        h_out(2, t)
+            for t in range(t0, t1):
+                if c == 0 and t < 2:
+                    gather_v(pa[c][:, t, :], h_rows[t], n3_t, c)
+                else:
+                    gather_s(pa[c][:, t, :], h_rows[t], n3_t, c)
+            with_h(u)
+            for t in range(t0, t1):
+                gather_s(pb[c][:, t, :], h_rows[t], n4_t, c)
+            if u == 3:
+                weave(nc.scalar.copy, o_woven[0][:], res[0][:])
+                weave(nc.scalar.copy, o_woven[1][:], res[1][:])
+            if u < 3:
+                finish(c, t0, t1, nc.vector)
+        finish(2, 0, 4, nc.vector)
+        planes_out(0)
         planes_out(1)
+        weave(nc.vector.tensor_copy, o_woven[2][:], res[2][:])
+        planes_out(2)
         for q in range(4):
             queue = nc.sync if q % 2 == 0 else nc.scalar
             queue.dma_start(out_2[0, 4 * q : 4 * q + 4, :].bitcast(I32), o_bytes[32 * q : 32 * q + 4, :].bitcast(I32))

@@ -14,12 +14,16 @@ ACT = mybir.ActivationFunctionType
 
 P = 128
 PACK = 4
-T, G, S = 1024, 2048, 512
-HALF = S // 2
-STARTS = (0, 256, 384)
-WIDTHS = (256, 128, 128)
-UNITS = ((0, 0, 2), (0, 2, 4), (1, 0, 4), (2, 0, 4))
-FLOPS = 3 * 2 * 512 * 512 * 512
+GROUP = 16
+BLOCKS = 16
+TOKENS, CODEWORDS = 1024, 2048
+S = 512
+LINE = 4
+
+CHUNKS = ((0, 256), (256, 128), (384, 128))
+PIECES = ((0, 0, 2), (0, 2, 4), (1, 0, 4), (2, 0, 4))
+
+FLOPS = 3 * 2 * S * S * S
 
 
 def tile_picked_twpqjointbrange_none_po_kernel(
@@ -31,248 +35,222 @@ def tile_picked_twpqjointbrange_none_po_kernel(
         keep = ctx.enter_context(tc.tile_pool(name="keep", bufs=1))
         psum = ctx.enter_context(tc.psum_pool(name="psum", bufs=1))
 
-        def sb(name, shape, dtype, tag=None):
-            return keep.tile(shape, dtype, name=name, tag=tag or name, align_bytes=64)
+        def sb(name, shape, dtype, reuse=None):
+            return keep.tile(shape, dtype, name=name, tag=reuse or name, align_bytes=64)
+
+        def by_chunk(name, dtype):
+            return [sb(name + str(c), [P, PACK, width], dtype) for c, (start, width) in enumerate(CHUNKS)]
 
         def load_list(name, src):
-            lst = keep.tile([P, S // 16], U16, name=name)
+            lst = keep.tile([P, S // GROUP], U16, name=name)
             nc.sync.dma_start(lst[:], src)
             return lst
 
-        def load_words(name, src, cols, tag=None):
-            words = sb(name, [P, cols], U32, tag)
+        def load_words(name, src, cols, reuse=None):
+            words = sb(name, [P, cols], U32, reuse)
             nc.sync.dma_start(words[:].bitcast(I32), src[0].rearrange("p n t -> p (n t)").bitcast(I32))
             return words
 
-        def load_block_rows(name, src, cols):
-            plane = sb(name, [P, cols], U8)
-            rows = src[0].bitcast(I32).unsqueeze(1).to_broadcast([16, 8, cols // 4])
-            nc.sync.dma_start(plane[:].bitcast(I32), rows)
-            return plane
+        def load_block_scales(name, src, cols):
+            table = sb(name, [P, cols], U8)
+            rows = src[0].bitcast(I32).unsqueeze(1).to_broadcast([BLOCKS, P // BLOCKS, cols // 4])
+            nc.sync.dma_start(table[:].bitcast(I32), rows)
+            return table
 
         two_t = load_list("two_t", two)
-        x_bytes = load_block_rows("x_bytes", x_scales, T)
+        x_bytes = load_block_scales("x_bytes", x_scales, TOKENS)
         k2_t = load_list("k2_t", k2)
-        d_bytes = load_block_rows("d_bytes", d_scales, G)
+        d_bytes = load_block_scales("d_bytes", d_scales, CODEWORDS)
         k1_t = load_list("k1_t", k1)
         offs_t = load_list("offs_t", offs)
-        x_w = load_words("x_w", x_words, T)
-        d_w = load_words("d_w", d_words, G)
+        x_w = load_words("x_w", x_words, TOKENS)
+        d_w = load_words("d_w", d_words, CODEWORDS)
         n1_t = load_list("n1_t", n1)
         n2_t = load_list("n2_t", n2)
         n3_t = load_list("n3_t", n3)
         n4_t = load_list("n4_t", n4)
 
+        gain_raw = sb("gain_raw", [P, PACK], F32)
+        nc.gpsimd.dma_start(gain_raw[:], gn.rearrange("(p t) o -> p (t o)", t=PACK))
+        gain = sb("gain", [P, PACK], F32)
+        nc.gpsimd.tensor_scalar(gain[:], gain_raw[:], 0.0625, 0.0, ALU.mult, ALU.add)
 
-        def deal(copy, dst, src):
-            copy(dst.rearrange("p (t m) -> p t m", t=PACK), src.rearrange("p (m t) -> p t m", t=PACK))
+        def deal_bytes(dst, src):
+            nc.vector.tensor_copy(dst.rearrange("p (t m) -> p t m", t=PACK), src.rearrange("p (m t) -> p t m", t=PACK))
 
         def deal_words(copy, dst, src):
             copy(dst.rearrange("p t m -> p m t"), src.rearrange("p (m t) -> p m t", t=PACK))
 
-        def half_of(lst, c):
-            return lst[:, c * HALF // 16 : (c + 1) * HALF // 16]
-
-        def scale_plane(name, d_list, x_list, tag):
-            picked = sb(name + "_picked", [P, 2 * S], U8, tag)
+        def scale_plane(name, d_list, x_list, reuse=None):
+            picked = sb(name + "_picked", [P, 2 * S], U8, reuse)
             plane = sb(name + "_plane", [P, 2 * S], U8)
             nc.vector.tensor_copy(picked[:, S:], x_bytes[:].indirect(x_list[:]))
             nc.vector.tensor_copy(picked[:, :S], d_bytes[:].indirect(d_list[:]))
             nc.vector.tensor_copy(plane[:, S:].bitcast(I32), picked[:, S:].bitcast(I32))
-            deal(nc.vector.tensor_copy, plane[:, :S], picked[:, :S])
+            deal_bytes(plane[:, :S], picked[:, :S])
             for r in range(1, 4):
                 nc.sync.dma_start(plane[r:P:32, :].bitcast(I32), plane[8 * r : P : 32, :].bitcast(I32))
             return plane
 
-        def products(name, d_dealt, x_picked, plane):
+        def coded_product(name, d_dealt, x_picked, plane):
             banks = []
             for t in range(PACK):
                 bank = psum.tile([P, S], F32, name=name + "_bank", tag=name + str(t))
-                cols = slice(t * P, (t + 1) * P)
                 nc.tensor.matmul_mx(
-                    bank[:], lhsT=d_dealt[:, cols].bitcast(FP8X4), lhsT_scale=plane[:, cols],
+                    bank[:], lhsT=d_dealt[:, t, :].bitcast(FP8X4), lhsT_scale=plane[:, t * P : (t + 1) * P],
                     rhs=x_picked.bitcast(FP8X4), rhs_scale=plane[:, S:], start=True, stop=True,
                 )
                 banks.append(bank)
             return banks
 
-        b_plane = scale_plane("b", k2_t, two_t, "b_picked")
-        w1_w = load_words("w1_w", w1_words, S, "b_picked")
+        b_plane = scale_plane("b", k2_t, two_t)
+        w1_w = load_words("w1_w", w1_words, S, reuse="b_picked")
         b_x = sb("b_x", [P, S], U32)
         nc.vector.tensor_copy(b_x[:], x_w[:].indirect(two_t[:]))
+        b_d = [sb("b_d" + str(half), [P, S // 2], U32) for half in range(2)]
         b_dealt = sb("b_dealt", [P, PACK, P], U32)
-        b_d = [sb("b_d" + str(c), [P, HALF], U32) for c in range(2)]
-        for c in range(2):
-            nc.vector.tensor_copy(b_d[c][:], d_w[:].indirect(half_of(k2_t, c)))
-        for c in range(2):
-            deal_words(nc.vector.tensor_copy, b_dealt[:, :, c * P // 2 : (c + 1) * P // 2], b_d[c][:])
-        b_banks = products("b", b_dealt[:].rearrange("p t m -> p (t m)"), b_x[:], b_plane)
+        for half in range(2):
+            nc.vector.tensor_copy(b_d[half][:], d_w[:].indirect(k2_t[:, half * GROUP : (half + 1) * GROUP]))
+        for half in range(2):
+            deal_words(nc.vector.tensor_copy, b_dealt[:, :, half * P // 2 : (half + 1) * P // 2], b_d[half][:])
+        b_banks = coded_product("b", b_dealt, b_x[:], b_plane)
 
-
-        w1_bytes = sb("w1_bytes", [P, S], U8, "b_x")
+        w1_dealt = sb("w1_dealt", [P, PACK, P], U32)
+        deal_words(nc.scalar.copy, w1_dealt[:], w1_w[:])
+        w1_bytes = sb("w1_bytes", [P, S], U8, reuse="b_x")
         nc.gpsimd.memset(w1_bytes[:].bitcast(I32), 0)
         for q in range(4):
             nc.sync.dma_start(w1_bytes[32 * q : 32 * q + 4, :].bitcast(I32), w1_scales[0, 4 * q : 4 * q + 4, :].bitcast(I32))
-        gain_raw = sb("gain_raw", [P, PACK], F32, "b_dealt")
-        nc.sync.dma_start(gain_raw[:], gn.rearrange("(p t) o -> p (t o)", t=PACK))
-        gain = sb("gain", [P, PACK], F32)
-        nc.gpsimd.tensor_scalar(gain[:], gain_raw[:], 0.0625, 0.0, ALU.mult, ALU.add)
 
-        a_plane = scale_plane("a", k1_t, offs_t, "b_d0")
-        a_words = sb("a_words", [P, 2 * S], U32, "b_d1")
-        a_dealt = sb("a_dealt", [P, S], U32)
+        a_plane = scale_plane("a", k1_t, offs_t, reuse="b_d0")
+        a_words = sb("a_words", [P, 2 * S], U32, reuse="b_d1")
+        a_dealt = sb("a_dealt", [P, PACK, P], U32)
         nc.vector.tensor_copy(a_words[:, :S], d_w[:].indirect(k1_t[:]))
         nc.vector.tensor_copy(a_words[:, S:], x_w[:].indirect(offs_t[:]))
-        deal_words(nc.vector.tensor_copy, a_dealt[:].rearrange("p (t m) -> p t m", t=PACK), a_words[:, :S])
-        a_banks = products("a", a_dealt[:], a_words[:, S:], a_plane)
+        deal_words(nc.vector.tensor_copy, a_dealt[:], a_words[:, :S])
+        a_banks = coded_product("a", a_dealt, a_words[:, S:], a_plane)
 
         def cols_of(c):
-            return slice(STARTS[c], STARTS[c] + WIDTHS[c])
+            return slice(CHUNKS[c][0], CHUNKS[c][0] + CHUNKS[c][1])
 
-        def entries(lst, c):
-            return lst[:, STARTS[c] // 16 : (STARTS[c] + WIDTHS[c]) // 16]
-
-        def gather_s(dst, window, lst, c):
-            nc.scalar.activation(dst, window[:].indirect(entries(lst, c)), ACT.Copy)
-
-        def gather_v(dst, window, lst, c):
-            nc.vector.tensor_copy(dst, window[:].indirect(entries(lst, c)))
-
-        def by_chunk(name, dtype):
-            return [sb(name + str(c), [P, PACK, WIDTHS[c]], dtype) for c in range(3)]
-
-        b_rows = [sb("b_row" + str(t), [P, S], F32) for t in range(PACK)]
-        g1 = by_chunk("g1_", F32)
-        g2, diff, th = by_chunk("g2_", F32), by_chunk("diff", F32), by_chunk("th", F32)
-        z_rows = by_chunk("z_rows", BF16)
-        z_woven = [sb("z_woven" + str(c), [P, WIDTHS[c], PACK], BF16) for c in range(3)]
-        z_codes = [sb("z_codes" + str(c), [P, WIDTHS[c]], U32) for c in range(3)]
-        z_bytes = [sb("z_bytes" + str(c), [P, WIDTHS[c]], U8) for c in range(3)]
+        def looked_up(rows, lst, c):
+            start, width = CHUNKS[c]
+            return rows[:].indirect(lst[:, start // GROUP : (start + width) // GROUP])
 
         def weave(copy, dst, src):
-            copy(dst.rearrange("p (c i) t -> p c t i", i=4), src.rearrange("p t (c i) -> p c t i", i=4))
+            copy(dst[:].rearrange("p (c i) t -> p c t i", i=LINE), src[:].rearrange("p t (c i) -> p c t i", i=LINE))
 
         def quantize(codes, plane, woven):
             nc.vector.quantize_mx(codes.bitcast(FP8X4), plane, woven[:].rearrange("p j t -> p (j t)"))
 
-        def sub_fused(c, t):
-            nc.vector.tensor_tensor(diff[c][:, t, :], b_rows[t][:].indirect(entries(n1_t, c)), g2[c][:, t, :], ALU.subtract)
+        b_rows = [sb("b_row" + str(t), [P, S], F32) for t in range(PACK)]
+        at_n2, th = by_chunk("at_n2_", F32), by_chunk("th", F32)
+        diff = [sb("diff0", [P, PACK, CHUNKS[0][1]], F32), sb("diff1", [P, PACK, CHUNKS[1][1]], F32)]
+        z_rows = by_chunk("z_rows", BF16)
+        z_woven = [sb("z_woven" + str(c), [P, width, PACK], BF16) for c, (start, width) in enumerate(CHUNKS)]
+        z_codes = [sb("z_codes" + str(c), [P, width], U32) for c, (start, width) in enumerate(CHUNKS)]
+        z_bytes = [sb("z_bytes" + str(c), [P, width], U8) for c, (start, width) in enumerate(CHUNKS)]
 
-        def tanh(c, t0, t1):
+        def difference(c, t):
+            nc.scalar.activation(at_n2[c][:, t, :], looked_up(b_rows[t], n2_t, c), ACT.Copy)
+            nc.vector.tensor_tensor(diff[c][:, t, :], looked_up(b_rows[t], n1_t, c), at_n2[c][:, t, :], ALU.subtract)
+
+        def tanh_of(c, t0, t1):
             nc.scalar.activation(th[c][:, t0:t1, :], diff[c][:, t0:t1, :], ACT.Tanh, scale=0.0625)
 
-        def make_z(c, t0, t1):
-            for t in range(t0, t1):
+        def make_z(c):
+            for t in range(PACK):
                 nc.vector.scalar_tensor_tensor(
                     z_rows[c][:, t, :], a_banks[t][:, cols_of(c)], gain[:, t : t + 1], th[c][:, t, :], ALU.mult, ALU.mult,
                 )
 
-        h_banks = [psum.tile([P, t1 - t0, WIDTHS[c]], F32, name="h_bank", tag="b" + str(u)) for u, (c, t0, t1) in enumerate(UNITS)]
+        h_banks = [
+            psum.tile([P, t1 - t0, CHUNKS[c][1]], F32, name="h_bank", tag="b" + str(u)) for u, (c, t0, t1) in enumerate(PIECES)
+        ]
+        h_psum = {(c, t): h_banks[u][:, t - t0, :] for u, (c, t0, t1) in enumerate(PIECES) for t in range(t0, t1)}
         h_rows = [sb("h_row" + str(t), [P, S], F32) for t in range(PACK)]
 
-        def h_psum(c, t):
-            u = [k for k, (cc, t0, t1) in enumerate(UNITS) if cc == c and t0 <= t < t1][0]
-            return h_banks[u][:, t - UNITS[u][1], :]
-
-        def h_product(c):
-            quantize(z_codes[c][:], z_bytes[c][:], z_woven[c])
-            for t in range(PACK):
-                cols = slice(t * P, (t + 1) * P)
+        def h_product(c, t0, t1):
+            for t in range(t0, t1):
                 nc.tensor.matmul_mx(
-                    h_psum(c, t), lhsT=w1_dealt[:, cols].bitcast(FP8X4), lhsT_scale=w1_sdealt[:, cols],
+                    h_psum[c, t], lhsT=w1_dealt[:, t, :].bitcast(FP8X4), lhsT_scale=w1_plane[:, t * P : (t + 1) * P],
                     rhs=z_codes[c][:].bitcast(FP8X4), rhs_scale=z_bytes[c][:], start=True, stop=True,
                 )
 
-        def h_out(c, t):
-            nc.scalar.copy(h_rows[t][:, cols_of(c)], h_psum(c, t))
+        def h_out(copy, c, t0, t1):
+            for t in range(t0, t1):
+                copy(h_rows[t][:, cols_of(c)], h_psum[c, t])
 
-        pa, pb = by_chunk("pa", F32), by_chunk("pb", F32)
-        hi2, lo2, hi3, lo3, res = [by_chunk(n, F32) for n in ("hi2_", "lo2_", "hi3_", "lo3_", "res")]
-        o_woven = [sb("o_woven" + str(c), [P, WIDTHS[c], PACK], BF16) for c in range(3)]
-        o_codes = [sb("o_codes" + str(c), [P, WIDTHS[c]], U32) for c in range(3)]
+        for t in range(PACK):
+            nc.scalar.copy(b_rows[t][:], b_banks[t][:])
+            difference(0, t)
+        for t in range(PACK):
+            difference(1, t)
+        w1_plane = sb("w1_plane", [P, S], U8, reuse="at_n2_0")
+        deal_bytes(w1_plane[:], w1_bytes[:])
+        tanh_of(0, 0, 2)
+        tanh_of(0, 2, 4)
+        make_z(0)
+        weave(nc.scalar.copy, z_woven[0], z_rows[0])
+        quantize(z_codes[0][:], z_bytes[0][:], z_woven[0])
+        h_product(0, 0, PACK)
+        diff.append(sb("diff2", [P, PACK, CHUNKS[2][1]], F32, reuse="th0"))
+        difference(2, 0)
+        difference(2, 1)
+        tanh_of(1, 0, PACK)
+        difference(2, 2)
+        difference(2, 3)
+        make_z(1)
+        tanh_of(2, 0, 2)
+        tanh_of(2, 2, 4)
+        weave(nc.vector.tensor_copy, z_woven[1], z_rows[1])
+        quantize(z_codes[1][:], z_bytes[1][:], z_woven[1])
+        h_product(1, 0, PACK)
+        make_z(2)
+        weave(nc.vector.tensor_copy, z_woven[2], z_rows[2])
+        quantize(z_codes[2][:], z_bytes[2][:], z_woven[2])
+        h_out(nc.scalar.copy, 0, 0, PACK)
+        h_out(nc.scalar.copy, 1, 0, PACK)
+        h_product(2, 0, 2)
+        h_out(nc.vector.tensor_copy, 2, 0, 2)
+        h_product(2, 2, 4)
+
+        hi2, lo2, hi3, lo3, res = [by_chunk(name, F32) for name in ("hi2_", "lo2_", "hi3_", "lo3_", "res")]
+        o_codes = [sb("o_codes" + str(c), [P, width], U32) for c, (start, width) in enumerate(CHUNKS)]
         o_bytes = sb("o_bytes", [P, S], U8)
         out_rows = out_0.rearrange("(p t) j -> p t j", t=PACK)
         out_words = out_1[0].rearrange("p n t -> p (n t)").bitcast(I32)
 
-        def with_h(u):
-            c, t0, t1 = UNITS[u]
-            nc.vector.tensor_tensor(hi2[c][:, t0:t1, :], pa[c][:, t0:t1, :], h_banks[u][:], ALU.max)
-            nc.vector.tensor_tensor(lo2[c][:, t0:t1, :], pa[c][:, t0:t1, :], h_banks[u][:], ALU.min)
+        for u, (c, t0, t1) in enumerate(PIECES):
+            sets = slice(t0, t1)
+            pa = sb("pa", [P, t1 - t0, CHUNKS[c][1]], F32, reuse="pa" + str(u % 2))
+            pb = sb("pb", [P, t1 - t0, CHUNKS[c][1]], F32, reuse="pb" + str(u % 2))
+            if u == 1:
+                h_out(nc.scalar.copy, 2, t0, t1)
+            for t in range(t0, t1):
+                if u == 0:
+                    nc.vector.tensor_copy(pa[:, t - t0, :], looked_up(h_rows[t], n3_t, c))
+                else:
+                    nc.scalar.activation(pa[:, t - t0, :], looked_up(h_rows[t], n3_t, c), ACT.Copy)
+            nc.vector.tensor_tensor(hi2[c][:, sets, :], pa[:], h_banks[u][:], ALU.max)
+            nc.vector.tensor_tensor(lo2[c][:, sets, :], pa[:], h_banks[u][:], ALU.min)
+            for t in range(t0, t1):
+                nc.scalar.activation(pb[:, t - t0, :], looked_up(h_rows[t], n4_t, c), ACT.Copy)
+            if u == len(PIECES) - 1:
+                o_woven = [sb("o_woven" + str(k), [P, CHUNKS[k][1], PACK], BF16, reuse="h_row" + str(3 - k)) for k in range(2)]
+                for k in range(2):
+                    weave(nc.scalar.copy, o_woven[k], res[k])
+            nc.vector.tensor_tensor(lo3[c][:, sets, :], lo2[c][:, sets, :], pb[:], ALU.min)
+            nc.vector.tensor_tensor(hi3[c][:, sets, :], hi2[c][:, sets, :], pb[:], ALU.max)
+            nc.vector.scalar_tensor_tensor(res[c][:, sets, :], lo3[c][:, sets, :], -0.5, hi3[c][:, sets, :], ALU.mult, ALU.add)
+            nc.sync.dma_start(out_rows[:, sets, cols_of(c)], res[c][:, sets, :])
 
-        def finish(c, t0, t1, engine):
-            nc.vector.tensor_tensor(lo3[c][:, t0:t1, :], lo2[c][:, t0:t1, :], pb[c][:, t0:t1, :], ALU.min)
-            nc.vector.tensor_tensor(hi3[c][:, t0:t1, :], hi2[c][:, t0:t1, :], pb[c][:, t0:t1, :], ALU.max)
-            nc.vector.scalar_tensor_tensor(res[c][:, t0:t1, :], lo3[c][:, t0:t1, :], -0.5, hi3[c][:, t0:t1, :], ALU.mult, ALU.add)
-            nc.sync.dma_start(out_rows[:, t0:t1, cols_of(c)], res[c][:, t0:t1, :])
-
-        def planes_out(c):
+        for c in range(len(CHUNKS)):
+            if c == len(CHUNKS) - 1:
+                o_woven.append(sb("o_woven" + str(c), [P, CHUNKS[c][1], PACK], BF16))
+                weave(nc.vector.tensor_copy, o_woven[c], res[c])
             quantize(o_codes[c][:], o_bytes[:, cols_of(c)], o_woven[c])
             nc.sync.dma_start(out_words[:, cols_of(c)], o_codes[c][:].bitcast(I32))
-
-        for t in range(PACK):
-            nc.scalar.copy(b_rows[t][:], b_banks[t][:])
-            gather_s(g2[0][:, t, :], b_rows[t], n2_t, 0)
-            if t == 0:
-                gather_s(g1[0][:, t, :], b_rows[t], n1_t, 0)
-        nc.vector.tensor_tensor(diff[0][:, 0, :], g1[0][:, 0, :], g2[0][:, 0, :], ALU.subtract)
-        for t in range(1, PACK):
-            sub_fused(0, t)
-        for t in range(PACK):
-            gather_s(g2[1][:, t, :], b_rows[t], n2_t, 1)
-            sub_fused(1, t)
-        w1_sdealt = sb("w1_sdealt", [P, S], U8, "g1_0")
-        deal(nc.vector.tensor_copy, w1_sdealt[:], w1_bytes[:])
-        tanh(0, 0, 2)
-        tanh(0, 2, 4)
-        make_z(0, 0, 4)
-        for t in range(PACK):
-            gather_s(g2[2][:, t, :], b_rows[t], n2_t, 2)
-            gather_s(g1[2][:, t, :], b_rows[t], n1_t, 2)
-            if t == 1:
-                tanh(1, 0, 4)
-            if t % 2 == 1:
-                nc.vector.tensor_tensor(diff[2][:, t - 1 : t + 1, :], g1[2][:, t - 1 : t + 1, :], g2[2][:, t - 1 : t + 1, :], ALU.subtract)
-        weave(nc.vector.tensor_copy, z_woven[0][:], z_rows[0][:])
-        w1_dealt = sb("w1_dealt", [P, S], U32, "g2_1")
-        deal_words(nc.scalar.copy, w1_dealt[:].rearrange("p (t m) -> p t m", t=PACK), w1_w[:])
-        h_product(0)
-        make_z(1, 0, 4)
-        tanh(2, 0, 2)
-        tanh(2, 2, 4)
-        weave(nc.vector.tensor_copy, z_woven[1][:], z_rows[1][:])
-        h_product(1)
-        make_z(2, 0, 4)
-        weave(nc.vector.tensor_copy, z_woven[2][:], z_rows[2][:])
-        h_product(2)
-        for t in range(PACK):
-            h_out(0, t)
-
-        for u, (c, t0, t1) in enumerate(UNITS):
-            for t in range(t0, t1):
-                if c == 0:
-                    h_out(1, t)
-                    if u == 0:
-                        nc.vector.tensor_copy(h_rows[t][:, cols_of(2)], h_psum(2, t))
-                    else:
-                        h_out(2, t)
-            for t in range(t0, t1):
-                if c == 0 and t < 2:
-                    gather_v(pa[c][:, t, :], h_rows[t], n3_t, c)
-                else:
-                    gather_s(pa[c][:, t, :], h_rows[t], n3_t, c)
-            with_h(u)
-            for t in range(t0, t1):
-                gather_s(pb[c][:, t, :], h_rows[t], n4_t, c)
-            if u == 3:
-                weave(nc.scalar.copy, o_woven[0][:], res[0][:])
-                weave(nc.scalar.copy, o_woven[1][:], res[1][:])
-            if u < 3:
-                finish(c, t0, t1, nc.vector)
-        finish(2, 0, 4, nc.vector)
-        planes_out(0)
-        planes_out(1)
-        weave(nc.vector.tensor_copy, o_woven[2][:], res[2][:])
-        planes_out(2)
         for q in range(4):
             queue = nc.sync if q % 2 == 0 else nc.scalar
             queue.dma_start(out_2[0, 4 * q : 4 * q + 4, :].bitcast(I32), o_bytes[32 * q : 32 * q + 4, :].bitcast(I32))

from contextlib import ExitStack

import concourse.mybir as mybir

F32 = mybir.dt.float32
BF16 = mybir.dt.bfloat16
I32 = mybir.dt.int32
U32 = mybir.dt.uint32
U16 = mybir.dt.uint16
U8 = mybir.dt.uint8
FP8X4 = mybir.dt.float8_e4m3fn_x4
ALU = mybir.AluOpType
ACT = mybir.ActivationFunctionType

P = 128
PACK = 4
GROUP = 16
BLOCKS = 16
TOKENS, CODEWORDS = 1024, 2048
S = 512
LINE = 4

CHUNKS = ((0, 256), (256, 128), (384, 128))
PIECES = ((0, 0, 2), (0, 2, 4), (1, 0, 4), (2, 0, 4))

FLOPS = 3 * 2 * S * S * S


def tile_picked_twpqjointbrange_none_po_kernel(
    tc, x_words, x_scales, d_words, d_scales, gn, w1_words, w1_scales,
    offs, k1, two, k2, n1, n2, n3, n4, out_0, out_1, out_2,
):
    nc = tc.nc
    with ExitStack() as ctx:
        keep = ctx.enter_context(tc.tile_pool(name="keep", bufs=1))
        psum = ctx.enter_context(tc.psum_pool(name="psum", bufs=1))

        def sb(name, shape, dtype, reuse=None):
            return keep.tile(shape, dtype, name=name, tag=reuse or name, align_bytes=64)

        def by_chunk(name, dtype):
            return [sb(name + str(c), [P, PACK, width], dtype) for c, (start, width) in enumerate(CHUNKS)]

        def load_list(name, src):
            lst = keep.tile([P, S // GROUP], U16, name=name)
            nc.sync.dma_start(lst[:], src)
            return lst

        def load_words(name, src, cols, reuse=None):
            words = sb(name, [P, cols], U32, reuse)
            nc.sync.dma_start(words[:].bitcast(I32), src[0].rearrange("p n t -> p (n t)").bitcast(I32))
            return words

        def load_block_scales(name, src, cols):
            table = sb(name, [P, cols], U8)
            rows = src[0].bitcast(I32).unsqueeze(1).to_broadcast([BLOCKS, P // BLOCKS, cols // 4])
            nc.sync.dma_start(table[:].bitcast(I32), rows)
            return table

        two_t = load_list("two_t", two)
        x_bytes = load_block_scales("x_bytes", x_scales, TOKENS)
        k2_t = load_list("k2_t", k2)
        d_bytes = load_block_scales("d_bytes", d_scales, CODEWORDS)
        k1_t = load_list("k1_t", k1)
        offs_t = load_list("offs_t", offs)
        x_w = load_words("x_w", x_words, TOKENS)
        d_w = load_words("d_w", d_words, CODEWORDS)
        n1_t = load_list("n1_t", n1)
        n2_t = load_list("n2_t", n2)
        n3_t = load_list("n3_t", n3)
        n4_t = load_list("n4_t", n4)

        gain_raw = sb("gain_raw", [P, PACK], F32)
        nc.gpsimd.dma_start(gain_raw[:], gn.rearrange("(p t) o -> p (t o)", t=PACK))
        gain = sb("gain", [P, PACK], F32)
        nc.gpsimd.tensor_scalar(gain[:], gain_raw[:], 0.0625, 0.0, ALU.mult, ALU.add)

        def deal_bytes(dst, src):
            nc.vector.tensor_copy(dst.rearrange("p (t m) -> p t m", t=PACK), src.rearrange("p (m t) -> p t m", t=PACK))

        def deal_words(copy, dst, src):
            copy(dst.rearrange("p t m -> p m t"), src.rearrange("p (m t) -> p m t", t=PACK))

        def scale_plane(name, d_list, x_list, reuse=None):
            picked = sb(name + "_picked", [P, 2 * S], U8, reuse)
            plane = sb(name + "_plane", [P, 2 * S], U8)
            nc.vector.tensor_copy(picked[:, S:], x_bytes[:].indirect(x_list[:]))
            nc.vector.tensor_copy(picked[:, :S], d_bytes[:].indirect(d_list[:]))
            nc.vector.tensor_copy(plane[:, S:].bitcast(I32), picked[:, S:].bitcast(I32))
            deal_bytes(plane[:, :S], picked[:, :S])
            for r in range(1, 4):
                nc.sync.dma_start(plane[r:P:32, :].bitcast(I32), plane[8 * r : P : 32, :].bitcast(I32))
            return plane

        def coded_product(name, d_dealt, x_picked, plane):
            banks = []
            for t in range(PACK):
                bank = psum.tile([P, S], F32, name=name + "_bank", tag=name + str(t))
                nc.tensor.matmul_mx(
                    bank[:], lhsT=d_dealt[:, t, :].bitcast(FP8X4), lhsT_scale=plane[:, t * P : (t + 1) * P],
                    rhs=x_picked.bitcast(FP8X4), rhs_scale=plane[:, S:], start=True, stop=True,
                )
                banks.append(bank)
            return banks

        b_plane = scale_plane("b", k2_t, two_t)
        w1_w = load_words("w1_w", w1_words, S, reuse="b_picked")
        b_x = sb("b_x", [P, S], U32)
        nc.vector.tensor_copy(b_x[:], x_w[:].indirect(two_t[:]))
        b_d = [sb("b_d" + str(half), [P, S // 2], U32) for half in range(2)]
        b_dealt = sb("b_dealt", [P, PACK, P], U32)
        for half in range(2):
            nc.vector.tensor_copy(b_d[half][:], d_w[:].indirect(k2_t[:, half * GROUP : (half + 1) * GROUP]))
        for half in range(2):
            deal_words(nc.vector.tensor_copy, b_dealt[:, :, half * P // 2 : (half + 1) * P // 2], b_d[half][:])
        b_banks = coded_product("b", b_dealt, b_x[:], b_plane)

        w1_dealt = sb("w1_dealt", [P, PACK, P], U32)
        deal_words(nc.scalar.copy, w1_dealt[:], w1_w[:])
        w1_bytes = sb("w1_bytes", [P, S], U8, reuse="b_x")
        nc.gpsimd.memset(w1_bytes[:].bitcast(I32), 0)
        for q in range(4):
            nc.sync.dma_start(w1_bytes[32 * q : 32 * q + 4, :].bitcast(I32), w1_scales[0, 4 * q : 4 * q + 4, :].bitcast(I32))

        a_plane = scale_plane("a", k1_t, offs_t, reuse="b_d0")
        a_words = sb("a_words", [P, 2 * S], U32, reuse="b_d1")
        a_dealt = sb("a_dealt", [P, PACK, P], U32)
        nc.vector.tensor_copy(a_words[:, :S], d_w[:].indirect(k1_t[:]))
        nc.vector.tensor_copy(a_words[:, S:], x_w[:].indirect(offs_t[:]))
        deal_words(nc.vector.tensor_copy, a_dealt[:], a_words[:, :S])
        a_banks = coded_product("a", a_dealt, a_words[:, S:], a_plane)

        def cols_of(c):
            return slice(CHUNKS[c][0], CHUNKS[c][0] + CHUNKS[c][1])

        def looked_up(rows, lst, c):
            start, width = CHUNKS[c]
            return rows[:].indirect(lst[:, start // GROUP : (start + width) // GROUP])

        def weave(copy, dst, src):
            copy(dst[:].rearrange("p (c i) t -> p c t i", i=LINE), src[:].rearrange("p t (c i) -> p c t i", i=LINE))

        def quantize(codes, plane, woven):
            nc.vector.quantize_mx(codes.bitcast(FP8X4), plane, woven[:].rearrange("p j t -> p (j t)"))

        b_rows = [sb("b_row" + str(t), [P, S], F32) for t in range(PACK)]
        at_n2, th = by_chunk("at_n2_", F32), by_chunk("th", F32)
        diff = [sb("diff0", [P, PACK, CHUNKS[0][1]], F32), sb("diff1", [P, PACK, CHUNKS[1][1]], F32)]
        z_rows = by_chunk("z_rows", BF16)
        z_woven = [sb("z_woven" + str(c), [P, width, PACK], BF16) for c, (start, width) in enumerate(CHUNKS)]
        z_codes = [sb("z_codes" + str(c), [P, width], U32) for c, (start, width) in enumerate(CHUNKS)]
        z_bytes = [sb("z_bytes" + str(c), [P, width], U8) for c, (start, width) in enumerate(CHUNKS)]

        def difference(c, t):
            nc.scalar.activation(at_n2[c][:, t, :], looked_up(b_rows[t], n2_t, c), ACT.Copy)
            nc.vector.tensor_tensor(diff[c][:, t, :], looked_up(b_rows[t], n1_t, c), at_n2[c][:, t, :], ALU.subtract)

        def tanh_of(c, t0, t1):
            nc.scalar.activation(th[c][:, t0:t1, :], diff[c][:, t0:t1, :], ACT.Tanh, scale=0.0625)

        def make_z(c):
            for t in range(PACK):
                nc.vector.scalar_tensor_tensor(
                    z_rows[c][:, t, :], a_banks[t][:, cols_of(c)], gain[:, t : t + 1], th[c][:, t, :], ALU.mult, ALU.mult,
                )

        h_banks = [
            psum.tile([P, t1 - t0, CHUNKS[c][1]], F32, name="h_bank", tag="b" + str(u)) for u, (c, t0, t1) in enumerate(PIECES)
        ]
        h_psum = {(c, t): h_banks[u][:, t - t0, :] for u, (c, t0, t1) in enumerate(PIECES) for t in range(t0, t1)}
        h_rows = [sb("h_row" + str(t), [P, S], F32) for t in range(PACK)]

        def h_product(c, t0, t1):
            for t in range(t0, t1):
                nc.tensor.matmul_mx(
                    h_psum[c, t], lhsT=w1_dealt[:, t, :].bitcast(FP8X4), lhsT_scale=w1_plane[:, t * P : (t + 1) * P],
                    rhs=z_codes[c][:].bitcast(FP8X4), rhs_scale=z_bytes[c][:], start=True, stop=True,
                )

        def h_out(copy, c, t0, t1):
            for t in range(t0, t1):
                copy(h_rows[t][:, cols_of(c)], h_psum[c, t])

        for t in range(PACK):
            nc.scalar.copy(b_rows[t][:], b_banks[t][:])
            difference(0, t)
        for t in range(PACK):
            difference(1, t)
        w1_plane = sb("w1_plane", [P, S], U8, reuse="at_n2_0")
        deal_bytes(w1_plane[:], w1_bytes[:])
        tanh_of(0, 0, 2)
        tanh_of(0, 2, 4)
        make_z(0)
        weave(nc.scalar.copy, z_woven[0], z_rows[0])
        quantize(z_codes[0][:], z_bytes[0][:], z_woven[0])
        h_product(0, 0, PACK)
        diff.append(sb("diff2", [P, PACK, CHUNKS[2][1]], F32, reuse="th0"))
        difference(2, 0)
        difference(2, 1)
        tanh_of(1, 0, PACK)
        difference(2, 2)
        difference(2, 3)
        make_z(1)
        tanh_of(2, 0, 2)
        tanh_of(2, 2, 4)
        weave(nc.vector.tensor_copy, z_woven[1], z_rows[1])
        quantize(z_codes[1][:], z_bytes[1][:], z_woven[1])
        h_product(1, 0, PACK)
        make_z(2)
        weave(nc.vector.tensor_copy, z_woven[2], z_rows[2])
        quantize(z_codes[2][:], z_bytes[2][:], z_woven[2])
        h_out(nc.scalar.copy, 0, 0, PACK)
        h_out(nc.scalar.copy, 1, 0, PACK)
        h_product(2, 0, 2)
        h_out(nc.vector.tensor_copy, 2, 0, 2)
        h_product(2, 2, 4)

        hi2, lo2, hi3, lo3, res = [by_chunk(name, F32) for name in ("hi2_", "lo2_", "hi3_", "lo3_", "res")]
        o_codes = [sb("o_codes" + str(c), [P, width], U32) for c, (start, width) in enumerate(CHUNKS)]
        o_bytes = sb("o_bytes", [P, S], U8)
        out_rows = out_0.rearrange("(p t) j -> p t j", t=PACK)
        out_words = out_1[0].rearrange("p n t -> p (n t)").bitcast(I32)

        for u, (c, t0, t1) in enumerate(PIECES):
            sets = slice(t0, t1)
            pa = sb("pa", [P, t1 - t0, CHUNKS[c][1]], F32, reuse="pa" + str(u % 2))
            pb = sb("pb", [P, t1 - t0, CHUNKS[c][1]], F32, reuse="pb" + str(u % 2))
            if u == 1:
                h_out(nc.scalar.copy, 2, t0, t1)
            for t in range(t0, t1):
                if u == 0:
                    nc.vector.tensor_copy(pa[:, t - t0, :], looked_up(h_rows[t], n3_t, c))
                else:
                    nc.scalar.activation(pa[:, t - t0, :], looked_up(h_rows[t], n3_t, c), ACT.Copy)
            nc.vector.tensor_tensor(hi2[c][:, sets, :], pa[:], h_banks[u][:], ALU.max)
            nc.vector.tensor_tensor(lo2[c][:, sets, :], pa[:], h_banks[u][:], ALU.min)
            for t in range(t0, t1):
                nc.scalar.activation(pb[:, t - t0, :], looked_up(h_rows[t], n4_t, c), ACT.Copy)
            if u == len(PIECES) - 1:
                o_woven = [sb("o_woven" + str(k), [P, CHUNKS[k][1], PACK], BF16, reuse="h_row" + str(3 - k)) for k in range(2)]
                for k in range(2):
                    weave(nc.scalar.copy, o_woven[k], res[k])
            nc.vector.tensor_tensor(lo3[c][:, sets, :], lo2[c][:, sets, :], pb[:], ALU.min)
            nc.vector.tensor_tensor(hi3[c][:, sets, :], hi2[c][:, sets, :], pb[:], ALU.max)
            nc.vector.scalar_tensor_tensor(res[c][:, sets, :], lo3[c][:, sets, :], -0.5, hi3[c][:, sets, :], ALU.mult, ALU.add)
            nc.sync.dma_start(out_rows[:, sets, cols_of(c)], res[c][:, sets, :])

        for c in range(len(CHUNKS)):
            if c == len(CHUNKS) - 1:
                o_woven.append(sb("o_woven" + str(c), [P, CHUNKS[c][1], PACK], BF16))
                weave(nc.vector.tensor_copy, o_woven[c], res[c])
            quantize(o_codes[c][:], o_bytes[:, cols_of(c)], o_woven[c])
            nc.sync.dma_start(out_words[:, cols_of(c)], o_codes[c][:].bitcast(I32))
        for q in range(4):
            queue = nc.sync if q % 2 == 0 else nc.scalar
            queue.dma_start(out_2[0, 4 * q : 4 * q + 4, :].bitcast(I32), o_bytes[32 * q : 32 * q + 4, :].bitcast(I32))
